import numpy as np
import ml_dtypes


def mxq(x, axis, fmt="e4m3"):
    dtype, down = {"e4m3": (ml_dtypes.float8_e4m3fn, 7), "e5m2": (ml_dtypes.float8_e5m2, 14)}[fmt]
    v = np.moveaxis(np.asarray(x, np.float32).astype(ml_dtypes.bfloat16).astype(np.float64), axis, -1)
    blocks = v.reshape(v.shape[:-1] + (-1, 32))
    amax = np.abs(blocks).max(-1, keepdims=True)
    byte = np.maximum(np.where(amax > 0, np.frexp(amax)[1] - 1 + 127, 0) - down, 1)
    scale = np.exp2(byte - 127.0)
    codes = (blocks / scale).astype(np.float32).astype(dtype).astype(np.float64)
    return np.moveaxis((codes * scale).reshape(v.shape), -1, axis)


WIDE = False


def mx_kscale(k):
    if not WIDE:
        return np.ones(k)
    levels = np.array([30, -30])
    if k % 512:
        return np.exp2(np.random.permutation(np.resize(levels, k // 32))).repeat(32)
    a = np.empty((k // 512, 16))
    for p in range(k // 512):
        a[p, :8] = np.random.permutation(np.resize(levels, 8))
        for g in range(8):
            far = levels[np.abs(levels - a[p, g]) >= 10]
            a[p, g + 8] = far[np.random.randint(len(far))]
    return np.exp2(a.ravel()).repeat(32)


def f64(x):
    return np.asarray(x).astype(np.float64)


def striped(idx):
    return np.tile(np.asarray(idx).reshape(-1, 16).T, (8, 1)).astype(np.uint16)


def unstriped(offs):
    return offs[:16].T.reshape(-1).astype(np.int64)


E2M1 = np.array([0.0, 0.5, 1.0, 1.5, 2.0, 3.0, 4.0, 6.0, -0.0, -0.5, -1.0, -1.5, -2.0, -3.0, -4.0, -6.0])


def pack_weight(w, fmt):
    k, n = w.shape
    w = f64(np.asarray(w, np.float32).astype(ml_dtypes.bfloat16)).reshape(k // 32, 32, n)
    amax = np.abs(w).max(1)
    if fmt == "e4m3":
        byte = np.frexp(amax)[1] - 1 + 127 - 7
    else:
        mant, ex = np.frexp(amax / 6.0)
        byte = np.where(mant > 0.5, ex, ex - 1) + 127
    byte = np.clip(np.where(amax > 0, byte, 1), 1, 254)
    scaled = (w * np.exp2(127.0 - byte)[:, None, :]).reshape(k, n).astype(np.float32)
    by_word = np.ascontiguousarray(scaled.reshape(k // 512, 128, 4, n).transpose(0, 1, 3, 2))
    if fmt == "e4m3":
        words = by_word.astype(ml_dtypes.float8_e4m3fn).view(np.uint8)
    else:
        c = by_word.astype(ml_dtypes.float4_e2m1fn).view(np.uint8) & 0xF
        words = (c[..., 0::2] | (c[..., 1::2] << 4)).reshape(k // 512, 128, 2 * n)
    return np.ascontiguousarray(words), np.ascontiguousarray(byte.astype(np.uint8).reshape(k // 512, 16, n))


def unpack_weight(words, scales, fmt):
    g, _, n = scales.shape
    words = np.ascontiguousarray(words).reshape(g, 128, n, -1)
    if fmt == "e4m3":
        vals = words.view(ml_dtypes.float8_e4m3fn).astype(np.float64)
    else:
        nib = np.empty((g, 128, n, 4), np.uint8)
        nib[..., 0::2] = words & 0xF
        nib[..., 1::2] = words >> 4
        vals = E2M1[nib]
    vals = vals * np.repeat(np.exp2(scales.astype(np.float64) - 127.0), 8, axis=1)[..., None]
    return vals.transpose(0, 1, 3, 2).reshape(g * 512, n)


def bf(x):
    return np.asarray(x, np.float32).astype(ml_dtypes.bfloat16)


def planes(Y):
    r, m = Y.shape
    b = f64(bf(Y)).reshape(r // 32, 32, m)
    amax = np.abs(b).max(1)
    byte = np.clip(np.where(amax > 0, np.frexp(amax)[1] - 1 + 127 - 7, 1), 1, 254)
    codes = (b * np.exp2(127.0 - byte)[:, None, :]).reshape(r, m).astype(np.float32).astype(ml_dtypes.float8_e4m3fn).view(np.uint8)
    words = codes.reshape(r // 512, 128, 4, m).transpose(0, 1, 3, 2)
    return np.ascontiguousarray(words), np.ascontiguousarray(byte.astype(np.uint8).reshape(r // 512, 16, m))


K, R, N, T, J = 512, 512, 512, 1024, 512


def setup_inputs():
    n = np.random.standard_normal
    idx = np.random.permutation(T)[:J]
    fk = mx_kscale(K)
    fr = mx_kscale(R)
    fn = mx_kscale(N)
    xtp = pack_weight(n((K, T)) / fk[:, None], "e2m1")
    wap = pack_weight(n((K, R)) * 1 / np.sqrt(K) * fk[:, None] * fr, "e4m3")
    wdp = pack_weight(n((N, R)) * 1 / np.sqrt(N) * fn[:, None], "e2m1")
    wup = pack_weight(n((R, K)) * 1 / np.sqrt(R) / fr[:, None], "e4m3")
    return {
        "xt_words": xtp[0],
        "xt_scales": xtp[1],
        "wa_words": wap[0],
        "wa_scales": wap[1],
        "g": (n((N, T)) * np.exp(0.5 * n((1, T))) / fn[:, None]).astype(np.float32),
        "wd_words": wdp[0],
        "wd_scales": wdp[1],
        "wu_words": wup[0],
        "wu_scales": wup[1],
        "run": (0.3 * n((K, T))).astype(np.float32),
        "offs": striped(idx),
    }


def reference(xt_words, xt_scales, wa_words, wa_scales, g, wd_words, wd_scales, wu_words, wu_scales, run, offs):
    idx = unstriped(offs)
    xtu = unpack_weight(xt_words, xt_scales, "e2m1")
    wau = unpack_weight(wa_words, wa_scales, "e4m3")
    wdu = unpack_weight(wd_words, wd_scales, "e2m1")
    wuu = unpack_weight(wu_words, wu_scales, "e4m3")
    xtidxg = xtu[:, idx]
    a = wau.T @ xtidxg
    gidxq = mxq(f64(g)[:, idx], 0, "e5m2")
    d = wdu.T @ gidxq
    dz = 2.0 * d * np.maximum(a, 0.0)
    dzq = mxq(dz, 0, "e5m2")
    p = wuu.T @ dzq
    pp = np.zeros((K, T))
    pp[:, idx] = p
    y = pp + f64(run)
    words, scales = planes(y)
    return y, words, scales

@@ -1,0 +1,257 @@
+from contextlib import ExitStack
+
+import concourse.mybir as mybir
+from concourse.masks import make_identity
+
+K, R, N, T, J = 512, 512, 512, 1024, 512
+FLOPS = 2 * J * (K * R + N * R + R * K)
+
+F32 = mybir.dt.float32
+BF16 = mybir.dt.bfloat16
+I32 = mybir.dt.int32
+U32 = mybir.dt.uint32
+U16 = mybir.dt.uint16
+U8 = mybir.dt.uint8
+E4M3 = mybir.dt.float8_e4m3fn_x4
+E5M2 = mybir.dt.float8_e5m2_x4
+E2M1 = mybir.dt.float4_e2m1fn_x4
+ALU = mybir.AluOpType
+ACT = mybir.ActivationFunctionType
+
+P = 128
+PACK = 4
+TOK = 128
+TILES = J // TOK
+CHUNK = 256
+CHUNKS = T // CHUNK
+
+
+def tile_moe_expert_back_made_anew_pl_kernel(
+    tc, xt_words, xt_scales, wa_words, wa_scales, g, wd_words, wd_scales, wu_words, wu_scales, run, offs,
+    out_0, out_1, out_2,
+):
+    nc = tc.nc
+    with ExitStack() as ctx:
+        keep = ctx.enter_context(tc.tile_pool(name="keep", bufs=1))
+        psum = ctx.enter_context(tc.psum_pool(name="psum", bufs=2))
+
+        def load_scales(plane, rows, queue=nc.sync):
+            for q in range(4):
+                queue.dma_start(
+                    out=plane[32 * q : 32 * q + 4, :].bitcast(I32), in_=rows[0, 4 * q : 4 * q + 4, :].bitcast(I32)
+                )
+
+        def load_scales_everywhere(plane, rows):
+            for q in range(4):
+                nc.sync.dma_start(
+                    out=plane[32 * q : 32 * q + 32, :].bitcast(I32),
+                    in_=rows[0, 4 * q : 4 * q + 4, :].bitcast(I32).partition_broadcast(8),
+                )
+
+        offsets = keep.tile([P, J // 16], U16, name="offsets")
+        xt_w = keep.tile([P, 2 * T], U8, name="xt_w", align_bytes=64)
+        xt_s = keep.tile([P, T], U8, name="xt_s", align_bytes=64)
+        w_s = keep.tile([P, 2 * R], U8, name="w_s", align_bytes=64)
+        wa_s, wd_s = (w_s[:, i * R : (i + 1) * R] for i in range(2))
+        wu_s = keep.tile([P, K], U8, name="wu_s", align_bytes=64)
+        wa_w = keep.tile([P, R], U32, name="wa_w", align_bytes=64)
+        wd_w = keep.tile([P, 2 * R], U8, name="wd_w", align_bytes=64)
+        wu_w = keep.tile([P, K], I32, name="wu_w", align_bytes=64)
+        g_rows = g.rearrange("(p t) c -> t p c", t=PACK)
+        run_rows = run.rearrange("(p t) c -> t p c", t=PACK)
+        out_rows = out_0.rearrange("(p t) c -> t p c", t=PACK)
+        g_low = keep.tile([P, 2, T], F32, name="g_low")
+        g_high = [keep.tile([P, T], F32, name="g_high%d" % t) for t in range(2)]
+        g_in = [g_low[:, 0, :], g_low[:, 1, :], g_high[0][:], g_high[1][:]]
+        run_in = [keep.tile([P, T], F32, name="run_in%d" % t) for t in range(PACK)]
+
+        nc.vector.memset(w_s[:].bitcast(I32), 0)
+
+        nc.sync.dma_start(offsets[:], offs)
+        nc.sync.dma_start(out=xt_w[:].bitcast(I32), in_=xt_words[0].bitcast(I32))
+        load_scales_everywhere(xt_s, xt_scales)
+        nc.sync.dma_start(out=g_low[:], in_=g.rearrange("(p t) c -> p t c", t=PACK)[:, 0:2, :])
+        nc.sync.dma_start(out=wa_w[:].bitcast(I32), in_=wa_words[0].rearrange("p c r -> p (c r)").bitcast(I32))
+        load_scales(wa_s, wa_scales)
+        nc.sync.dma_start(out=g_in[2], in_=g_rows[2])
+        nc.sync.dma_start(out=g_in[3], in_=g_rows[3])
+        nc.sync.dma_start(out=wd_w[:].bitcast(I32), in_=wd_words[0].bitcast(I32))
+        load_scales(wd_s, wd_scales)
+        nc.sync.dma_start(out=wu_w[:], in_=wu_words[0].rearrange("p c r -> p (c r)").bitcast(I32))
+        nc.gpsimd.memset(wu_s[:].bitcast(I32), 0)
+        load_scales(wu_s, wu_scales, nc.gpsimd)
+        for t in range(PACK):
+            nc.sync.dma_start(out=run_in[t][:], in_=run_rows[t])
+
+        ident = keep.tile([P, P], F32, name="ident")
+        make_identity(nc, ident[:])
+
+        placed = [keep.tile([P, T], F32, name="placed%d" % t) for t in range(PACK)]
+        for t in range(PACK):
+            nc.vector.memset(placed[t][:], 0.0)
+
+        xg_w = keep.tile([P, 2 * J], U8, name="xg_w", align_bytes=64)
+        xg_s = keep.tile([P, J], U8, name="xg_s", align_bytes=64)
+        nc.vector.tensor_copy(xg_w[:].bitcast(U16), xt_w[:].bitcast(U16).indirect(offsets[:]))
+        nc.vector.tensor_copy(xg_s[:], xt_s[:].indirect(offsets[:]))
+
+        relu2 = [keep.tile([P, R], F32, name="relu2_%d" % i) for i in range(TILES)]
+        for i in range(TILES):
+            a_ps = psum.tile([P, R], F32, name="a_ps")
+            nc.tensor.matmul_mx(
+                out=a_ps[:],
+                lhsT=xg_w[:, 2 * TOK * i : 2 * TOK * (i + 1)].bitcast(E2M1),
+                lhsT_scale=xg_s[:, TOK * i : TOK * (i + 1)],
+                rhs=wa_w[:].bitcast(E4M3),
+                rhs_scale=wa_s,
+                start=True,
+                stop=True,
+            )
+            nc.scalar.activation(
+                out=relu2[i][:],
+                in_=a_ps[:],
+                func=ACT.Relu,
+                scale=2.0,
+            )
+
+        g_pick = keep.tile([P, PACK, J], F32, name="g_pick", align_bytes=64)
+        for t in range(PACK - 1):
+            nc.vector.tensor_copy(g_pick[:, t, :], g_in[t].indirect(offsets[:]))
+
+        g_codes = keep.tile([P, J], U32, name="g_codes", align_bytes=64)
+        g_scales = keep.tile([P, J], U8, name="g_scales", align_bytes=64)
+        dz_codes = keep.tile([P, J], U32, name="dz_codes", align_bytes=64)
+        dz_scales = keep.tile([P, J], U8, name="dz_scales", align_bytes=64)
+        g_woven = [keep.tile([P, TOK, PACK], BF16, name="g_woven%d" % i, align_bytes=64) for i in range(TILES)]
+        dz_rows = [keep.tile([P, R], BF16, name="dz_rows%d" % i, align_bytes=64) for i in range(TILES)]
+        dz_woven = [keep.tile([P, TOK * PACK], BF16, name="dz_woven%d" % i, align_bytes=64) for i in range(TILES)]
+        d_ps = {}
+
+        def pick_last(i):
+            cols = slice(TOK * i, TOK * (i + 1))
+            nc.vector.tensor_copy(
+                g_pick[:, PACK - 1, cols], g_in[PACK - 1].indirect(offsets[:, 8 * i : 8 * (i + 1)])
+            )
+            weave = nc.vector.tensor_copy if i == 0 else nc.scalar.copy
+            weave(
+                out=g_woven[i][:].rearrange("p (c n) t -> p c t n", n=4),
+                in_=g_pick[:, :, cols].rearrange("p t (c n) -> p c t n", n=4),
+            )
+
+        def product_d(i):
+            cols = slice(TOK * i, TOK * (i + 1))
+            nc.vector.quantize_mx(
+                out=g_codes[:, cols].bitcast(E5M2),
+                scales=g_scales[:, cols],
+                in_=g_woven[i][:].rearrange("p j t -> p (j t)"),
+            )
+            d_ps[i] = psum.tile([P, R], F32, name="d_ps")
+            nc.tensor.matmul_mx(
+                out=d_ps[i][:],
+                lhsT=g_codes[:, cols].bitcast(E5M2),
+                lhsT_scale=g_scales[:, cols],
+                rhs=wd_w[:].bitcast(E2M1),
+                rhs_scale=wd_s,
+                start=True,
+                stop=True,
+            )
+
+        def make_dz(i):
+            nc.vector.tensor_tensor(
+                out=dz_rows[i][:],
+                in0=d_ps[i][:],
+                in1=relu2[i][:],
+                op=ALU.mult,
+            )
+            turned = psum.tile([P, 2, TOK], F32, name="turned")
+            words = dz_rows[i][:].bitcast(F32)
+            for u in range(2):
+                nc.tensor.transpose(turned[:, u, :], words[:, u : 2 * P : 2], ident[:])
+            nc.scalar.copy(
+                out=dz_woven[i][:].bitcast(F32).rearrange("p (j u) -> p j u", u=2),
+                in_=turned[:].rearrange("p u j -> p j u"),
+            )
+
+        def quantize_dz(i):
+            cols = slice(TOK * i, TOK * (i + 1))
+            nc.vector.quantize_mx(out=dz_codes[:, cols].bitcast(E5M2), scales=dz_scales[:, cols], in_=dz_woven[i][:])
+
+        wu_wp = keep.tile([P, K], I32, name="wu_wp", align_bytes=64)
+        wu_sp = keep.tile([P, K], U8, name="wu_sp", align_bytes=64)
+
+        for step in range(TILES + 3):
+            if step < TILES:
+                pick_last(step)
+            if 0 <= step - 1 < TILES:
+                product_d(step - 1)
+            if 0 <= step - 2 < TILES:
+                make_dz(step - 2)
+            if step == TILES + 2:
+                nc.vector.tensor_copy(
+                    out=wu_wp[:].rearrange("p (t m) -> p m t", t=PACK), in_=wu_w[:].rearrange("p (m t) -> p m t", t=PACK)
+                )
+                nc.vector.tensor_copy(
+                    out=wu_sp[:].rearrange("p (t m) -> p m t", t=PACK), in_=wu_s[:].rearrange("p (m t) -> p m t", t=PACK)
+                )
+            if 0 <= step - 3 < TILES:
+                quantize_dz(step - 3)
+
+        p_rows = [keep.tile([P, J], F32, name="p_rows%d" % t) for t in range(PACK)]
+        y_pair = [keep.tile([P, 2, T], F32, name="y_pair%d" % h) for h in range(2)]
+        y_woven = [keep.tile([P, CHUNK, PACK], BF16, name="y_woven%d" % c, align_bytes=64) for c in range(CHUNKS)]
+        y_codes = keep.tile([P, T], U32, name="y_codes", align_bytes=64)
+        y_scales = keep.tile([P, T], U8, name="y_scales", align_bytes=64)
+
+        for t in range(PACK):
+            p_ps = psum.tile([P, J], F32, name="p_ps")
+            nc.tensor.matmul_mx(
+                out=p_ps[:],
+                lhsT=wu_wp[:, P * t : P * (t + 1)].bitcast(E4M3),
+                lhsT_scale=wu_sp[:, P * t : P * (t + 1)],
+                rhs=dz_codes[:].bitcast(E5M2),
+                rhs_scale=dz_scales[:],
+                start=True,
+                stop=True,
+            )
+            nc.scalar.copy(out=p_rows[t][:], in_=p_ps[:])
+
+        def weave_pair(engine_copy, h, c):
+            cols = slice(CHUNK * c, CHUNK * (c + 1))
+            engine_copy(out=y_woven[c][:, :, 2 * h : 2 * h + 2], in_=y_pair[h][:, :, cols].rearrange("p t c -> p c t"))
+
+        for t in range(PACK):
+            nc.vector.tensor_copy(placed[t][:].indirect(offsets[:]), p_rows[t][:])
+            if t < PACK - 1:
+                y_t = y_pair[t // 2][:, t % 2, :]
+                nc.gpsimd.tensor_tensor(out=y_t, in0=placed[t][:], in1=run_in[t][:], op=ALU.add)
+                nc.sync.dma_start(out=out_rows[t], in_=y_t)
+            if t == 1:
+                for c in range(CHUNKS):
+                    weave_pair(nc.scalar.copy, 0, c)
+
+        last = PACK - 1
+        for c in range(CHUNKS):
+            cols = slice(CHUNK * c, CHUNK * (c + 1))
+            nc.vector.tensor_tensor(
+                out=y_pair[1][:, 1, cols], in0=placed[last][:, cols], in1=run_in[last][:, cols], op=ALU.add
+            )
+            if c % 2 == 1:
+                half = slice(CHUNK * (c - 1), CHUNK * (c + 1))
+                nc.sync.dma_start(out=out_rows[last][:, half], in_=y_pair[1][:, 1, half])
+        for c in range(CHUNKS):
+            weave_pair(nc.scalar.copy if c < CHUNKS // 2 else nc.vector.tensor_copy, 1, c)
+
+        words_out = out_1[0].rearrange("p c r -> p (c r)").bitcast(I32)
+        for c in (0, 2, 3, 1):
+            cols = slice(CHUNK * c, CHUNK * (c + 1))
+            nc.vector.quantize_mx(
+                out=y_codes[:, cols].bitcast(E4M3),
+                scales=y_scales[:, cols],
+                in_=y_woven[c][:].rearrange("p c t -> p (c t)"),
+            )
+            nc.sync.dma_start(out=words_out[:, cols], in_=y_codes[:, cols].bitcast(I32))
+        for q in range(4):
+            queue = nc.sync if q % 2 == 0 else nc.scalar
+            queue.dma_start(
+                out=out_2[0, 4 * q : 4 * q + 4, :].bitcast(I32), in_=y_scales[32 * q : 32 * q + 4, :].bitcast(I32)
+            )

@@ -22,6 +22,7 @@ P = 128
 PACK = 4
 TOK = 128
 TILES = J // TOK
+EARLY = 2 * TOK
 CHUNK = 256
 CHUNKS = T // CHUNK
 
@@ -34,12 +35,6 @@ def tile_moe_expert_back_made_anew_pl_kernel(
     with ExitStack() as ctx:
         keep = ctx.enter_context(tc.tile_pool(name="keep", bufs=1))
         psum = ctx.enter_context(tc.psum_pool(name="psum", bufs=2))
-
-        def load_scales(plane, rows, queue=nc.sync):
-            for q in range(4):
-                queue.dma_start(
-                    out=plane[32 * q : 32 * q + 4, :].bitcast(I32), in_=rows[0, 4 * q : 4 * q + 4, :].bitcast(I32)
-                )
 
         def load_scales_everywhere(plane, rows):
             for q in range(4):
@@ -60,43 +55,47 @@ def tile_moe_expert_back_made_anew_pl_kernel(
         g_rows = g.rearrange("(p t) c -> t p c", t=PACK)
         run_rows = run.rearrange("(p t) c -> t p c", t=PACK)
         out_rows = out_0.rearrange("(p t) c -> t p c", t=PACK)
-        g_low = keep.tile([P, 2, T], F32, name="g_low")
-        g_high = [keep.tile([P, T], F32, name="g_high%d" % t) for t in range(2)]
-        g_in = [g_low[:, 0, :], g_low[:, 1, :], g_high[0][:], g_high[1][:]]
+        g_in = [keep.tile([P, T], F32, name="g_in%d" % t) for t in range(PACK)]
         run_in = [keep.tile([P, T], F32, name="run_in%d" % t) for t in range(PACK)]
 
-        nc.vector.memset(w_s[:].bitcast(I32), 0)
 
         nc.sync.dma_start(offsets[:], offs)
-        nc.sync.dma_start(out=xt_w[:].bitcast(I32), in_=xt_words[0].bitcast(I32))
         load_scales_everywhere(xt_s, xt_scales)
-        nc.sync.dma_start(out=g_low[:], in_=g.rearrange("(p t) c -> p t c", t=PACK)[:, 0:2, :])
+        nc.sync.dma_start(out=xt_w[:].bitcast(I32), in_=xt_words[0].bitcast(I32))
         nc.sync.dma_start(out=wa_w[:].bitcast(I32), in_=wa_words[0].rearrange("p c r -> p (c r)").bitcast(I32))
-        load_scales(wa_s, wa_scales)
-        nc.sync.dma_start(out=g_in[2], in_=g_rows[2])
-        nc.sync.dma_start(out=g_in[3], in_=g_rows[3])
+        nc.sync.dma_start(out=g_in[0][:], in_=g_rows[0])
+        load_scales_everywhere(wa_s, wa_scales)
+        for t in range(1, PACK):
+            nc.sync.dma_start(out=g_in[t][:], in_=g_rows[t])
         nc.sync.dma_start(out=wd_w[:].bitcast(I32), in_=wd_words[0].bitcast(I32))
-        load_scales(wd_s, wd_scales)
+        load_scales_everywhere(wd_s, wd_scales)
         nc.sync.dma_start(out=wu_w[:], in_=wu_words[0].rearrange("p c r -> p (c r)").bitcast(I32))
-        nc.gpsimd.memset(wu_s[:].bitcast(I32), 0)
-        load_scales(wu_s, wu_scales, nc.gpsimd)
+        load_scales_everywhere(wu_s, wu_scales)
         for t in range(PACK):
             nc.sync.dma_start(out=run_in[t][:], in_=run_rows[t])
 
         ident = keep.tile([P, P], F32, name="ident")
         make_identity(nc, ident[:])
 
-        placed = [keep.tile([P, T], F32, name="placed%d" % t) for t in range(PACK)]
-        for t in range(PACK):
+        placed = [keep.tile([P, T], F32, name="placed%d" % t) for t in range(PACK - 1)]
+        for t in range(PACK - 1):
             nc.vector.memset(placed[t][:], 0.0)
 
         xg_w = keep.tile([P, 2 * J], U8, name="xg_w", align_bytes=64)
         xg_s = keep.tile([P, J], U8, name="xg_s", align_bytes=64)
-        nc.vector.tensor_copy(xg_w[:].bitcast(U16), xt_w[:].bitcast(U16).indirect(offsets[:]))
         nc.vector.tensor_copy(xg_s[:], xt_s[:].indirect(offsets[:]))
+        nc.vector.tensor_copy(xg_w[:].bitcast(U16), xt_w[:].bitcast(U16).indirect(offsets[:]))
 
-        relu2 = [keep.tile([P, R], F32, name="relu2_%d" % i) for i in range(TILES)]
-        for i in range(TILES):
+        g_pick = keep.tile([P, PACK, J], BF16, name="g_pick", align_bytes=64)
+        g_round = keep.tile([P, T], BF16, name="g_round", align_bytes=64)
+        nc.scalar.activation(out=g_round[:], in_=g_in[0][:], func=ACT.Copy)
+        nc.scalar.activation(out=g_pick[:, 0, :], in_=g_round[:].indirect(offsets[:]), func=ACT.Copy)
+
+        relu2 = {}
+
+        def product_a(i):
+            tag = "relu2_%d" % i if i < 2 else "g_woven%d" % (i - 2)
+            relu2[i] = keep.tile([P, R], F32, name="relu2_%d" % i, tag=tag, align_bytes=64)
             a_ps = psum.tile([P, R], F32, name="a_ps")
             nc.tensor.matmul_mx(
                 out=a_ps[:],
@@ -114,41 +113,45 @@ def tile_moe_expert_back_made_anew_pl_kernel(
                 scale=2.0,
             )
 
-        g_pick = keep.tile([P, PACK, J], F32, name="g_pick", align_bytes=64)
-        for t in range(PACK - 1):
-            nc.vector.tensor_copy(g_pick[:, t, :], g_in[t].indirect(offsets[:]))
+        product_a(0)
+        product_a(1)
 
-        g_codes = keep.tile([P, J], U32, name="g_codes", align_bytes=64)
+        for t in range(1, PACK - 1):
+            nc.vector.tensor_copy(g_pick[:, t, :], g_in[t][:].indirect(offsets[:]))
+
         g_scales = keep.tile([P, J], U8, name="g_scales", align_bytes=64)
-        dz_codes = keep.tile([P, J], U32, name="dz_codes", align_bytes=64)
-        dz_scales = keep.tile([P, J], U8, name="dz_scales", align_bytes=64)
-        g_woven = [keep.tile([P, TOK, PACK], BF16, name="g_woven%d" % i, align_bytes=64) for i in range(TILES)]
-        dz_rows = [keep.tile([P, R], BF16, name="dz_rows%d" % i, align_bytes=64) for i in range(TILES)]
-        dz_woven = [keep.tile([P, TOK * PACK], BF16, name="dz_woven%d" % i, align_bytes=64) for i in range(TILES)]
+        dz_codes = keep.tile([P, EARLY + J], U32, name="dz_codes", align_bytes=64)
+        dz_scales = keep.tile([P, EARLY + J], U8, name="dz_scales", align_bytes=64)
+        nc.vector.memset(dz_codes[:, 0:EARLY].bitcast(I32), 0)
+        nc.vector.memset(dz_scales[:, 0:EARLY].bitcast(I32), 0)
+        g_woven = [keep.tile([P, TOK, PACK], BF16, name="g_woven%d" % i, tag="g_woven%d" % i, align_bytes=64) for i in range(TILES)]
+        dz_rows = [keep.tile([P, R], BF16, name="dz_rows%d" % i, tag="dz_rows%d" % i, align_bytes=64) for i in range(TILES)]
+        dz_woven = [keep.tile([P, TOK * PACK], BF16, name="dz_woven%d" % i, tag="dz_woven%d" % i, align_bytes=64) for i in range(TILES)]
         d_ps = {}
 
         def pick_last(i):
             cols = slice(TOK * i, TOK * (i + 1))
             nc.vector.tensor_copy(
-                g_pick[:, PACK - 1, cols], g_in[PACK - 1].indirect(offsets[:, 8 * i : 8 * (i + 1)])
+                g_pick[:, PACK - 1, cols], g_in[PACK - 1][:].indirect(offsets[:, 8 * i : 8 * (i + 1)])
             )
-            weave = nc.vector.tensor_copy if i == 0 else nc.scalar.copy
-            weave(
+            nc.scalar.copy(
                 out=g_woven[i][:].rearrange("p (c n) t -> p c t n", n=4),
                 in_=g_pick[:, :, cols].rearrange("p t (c n) -> p c t n", n=4),
             )
 
         def product_d(i):
             cols = slice(TOK * i, TOK * (i + 1))
+            tag = "g_codes%d" % i if i < 2 else "relu2_%d" % (i - 2)
+            g_codes = keep.tile([P, TOK], U32, name="g_codes%d" % i, tag=tag, align_bytes=64)
             nc.vector.quantize_mx(
-                out=g_codes[:, cols].bitcast(E5M2),
+                out=g_codes[:].bitcast(E5M2),
                 scales=g_scales[:, cols],
                 in_=g_woven[i][:].rearrange("p j t -> p (j t)"),
             )
             d_ps[i] = psum.tile([P, R], F32, name="d_ps")
             nc.tensor.matmul_mx(
                 out=d_ps[i][:],
-                lhsT=g_codes[:, cols].bitcast(E5M2),
+                lhsT=g_codes[:].bitcast(E5M2),
                 lhsT_scale=g_scales[:, cols],
                 rhs=wd_w[:].bitcast(E2M1),
                 rhs_scale=wd_s,
@@ -173,57 +176,79 @@ def tile_moe_expert_back_made_anew_pl_kernel(
             )
 
         def quantize_dz(i):
-            cols = slice(TOK * i, TOK * (i + 1))
+            cols = slice(EARLY + TOK * i, EARLY + TOK * (i + 1))
             nc.vector.quantize_mx(out=dz_codes[:, cols].bitcast(E5M2), scales=dz_scales[:, cols], in_=dz_woven[i][:])
 
-        wu_wp = keep.tile([P, K], I32, name="wu_wp", align_bytes=64)
-        wu_sp = keep.tile([P, K], U8, name="wu_sp", align_bytes=64)
+        wu_dealt = {}
 
-        for step in range(TILES + 3):
-            if step < TILES:
-                pick_last(step)
-            if 0 <= step - 1 < TILES:
-                product_d(step - 1)
-            if 0 <= step - 2 < TILES:
-                make_dz(step - 2)
-            if step == TILES + 2:
-                nc.vector.tensor_copy(
-                    out=wu_wp[:].rearrange("p (t m) -> p m t", t=PACK), in_=wu_w[:].rearrange("p (m t) -> p m t", t=PACK)
-                )
-                nc.vector.tensor_copy(
-                    out=wu_sp[:].rearrange("p (t m) -> p m t", t=PACK), in_=wu_s[:].rearrange("p (m t) -> p m t", t=PACK)
-                )
-            if 0 <= step - 3 < TILES:
-                quantize_dz(step - 3)
+        def deal_wu():
+            wu_wp = keep.tile([P, K], I32, name="wu_wp", align_bytes=64)
+            wu_sp = keep.tile([P, K], U8, name="wu_sp", align_bytes=64)
+            nc.vector.tensor_copy(
+                out=wu_wp[:].rearrange("p (t m) -> p m t", t=PACK), in_=wu_w[:].rearrange("p (m t) -> p m t", t=PACK)
+            )
+            nc.vector.tensor_copy(
+                out=wu_sp[:].rearrange("p (t m) -> p m t", t=PACK), in_=wu_s[:].rearrange("p (m t) -> p m t", t=PACK)
+            )
+            wu_dealt["words"] = wu_wp
+            wu_dealt["scales"] = wu_sp
 
-        p_rows = [keep.tile([P, J], F32, name="p_rows%d" % t) for t in range(PACK)]
+        def product_p(t, first):
+            p_ps = psum.tile([P, J], F32, name="p_ps")
+            nc.tensor.matmul_mx(
+                out=p_ps[:],
+                lhsT=wu_dealt["words"][:, P * t : P * (t + 1)].bitcast(E4M3),
+                lhsT_scale=wu_dealt["scales"][:, P * t : P * (t + 1)],
+                rhs=dz_codes[:, first : first + J].bitcast(E5M2),
+                rhs_scale=dz_scales[:, first : first + J],
+                start=True,
+                stop=True,
+            )
+            return p_ps
+
+        def place(t, lo, hi, sums, tag):
+            rows = keep.tile([P, hi - lo], F32, name="p_rows%d_%d" % (t, lo), tag=tag, align_bytes=64)
+            nc.scalar.copy(out=rows[:], in_=sums)
+            nc.vector.tensor_copy(placed[t][:].indirect(offsets[:, lo // 16 : hi // 16]), rows[:])
+
+        for i in range(TILES):
+            pick_last(i)
+        product_d(0)
+        product_a(2)
+        product_d(1)
+        product_a(3)
+        deal_wu()
+        make_dz(0)
+        product_d(2)
+        make_dz(1)
+        product_d(3)
+        quantize_dz(0)
+        make_dz(2)
+        quantize_dz(1)
+        early = product_p(0, 0)
+        make_dz(3)
+        quantize_dz(2)
+        place(0, 0, TOK, early[:, EARLY : EARLY + TOK], "p_first")
+        quantize_dz(3)
+        placed.append(keep.tile([P, T], F32, name="placed3", tag="dz_woven3", align_bytes=64))
+        nc.vector.memset(placed[3][:], 0.0)
+        place(0, TOK, EARLY, early[:, EARLY + TOK : J], "dz_rows3")
+
         y_pair = [keep.tile([P, 2, T], F32, name="y_pair%d" % h) for h in range(2)]
         y_woven = [keep.tile([P, CHUNK, PACK], BF16, name="y_woven%d" % c, align_bytes=64) for c in range(CHUNKS)]
         y_codes = keep.tile([P, T], U32, name="y_codes", align_bytes=64)
         y_scales = keep.tile([P, T], U8, name="y_scales", align_bytes=64)
-
-        for t in range(PACK):
-            p_ps = psum.tile([P, J], F32, name="p_ps")
-            nc.tensor.matmul_mx(
-                out=p_ps[:],
-                lhsT=wu_wp[:, P * t : P * (t + 1)].bitcast(E4M3),
-                lhsT_scale=wu_sp[:, P * t : P * (t + 1)],
-                rhs=dz_codes[:].bitcast(E5M2),
-                rhs_scale=dz_scales[:],
-                start=True,
-                stop=True,
-            )
-            nc.scalar.copy(out=p_rows[t][:], in_=p_ps[:])
 
         def weave_pair(engine_copy, h, c):
             cols = slice(CHUNK * c, CHUNK * (c + 1))
             engine_copy(out=y_woven[c][:, :, 2 * h : 2 * h + 2], in_=y_pair[h][:, :, cols].rearrange("p t c -> p c t"))
 
         for t in range(PACK):
-            nc.vector.tensor_copy(placed[t][:].indirect(offsets[:]), p_rows[t][:])
+            lo = EARLY if t == 0 else 0
+            place(t, lo, J, product_p(t, EARLY)[:, lo:J], "p_rows%d" % t)
             if t < PACK - 1:
                 y_t = y_pair[t // 2][:, t % 2, :]
-                nc.gpsimd.tensor_tensor(out=y_t, in0=placed[t][:], in1=run_in[t][:], op=ALU.add)
+                nc.vector.tensor_tensor(out=y_t, in0=placed[t][:], in1=run_in[t][:], op=ALU.add)
                 nc.sync.dma_start(out=out_rows[t], in_=y_t)
             if t == 1:
                 for c in range(CHUNKS):

@@ -131,9 +131,6 @@ def tile_moe_expert_back_made_anew_pl_kernel(
 
         def pick_last(i):
             cols = slice(TOK * i, TOK * (i + 1))
-            nc.vector.tensor_copy(
-                g_pick[:, PACK - 1, cols], g_in[PACK - 1][:].indirect(offsets[:, 8 * i : 8 * (i + 1)])
-            )
             nc.scalar.copy(
                 out=g_woven[i][:].rearrange("p (c n) t -> p c t n", n=4),
                 in_=g_pick[:, :, cols].rearrange("p t (c n) -> p c t n", n=4),
@@ -211,6 +208,10 @@ def tile_moe_expert_back_made_anew_pl_kernel(
             nc.scalar.copy(out=rows[:], in_=sums)
             nc.vector.tensor_copy(placed[t][:].indirect(offsets[:, lo // 16 : hi // 16]), rows[:])
 
+        for lo, hi in ((0, TOK), (TOK, J)):
+            nc.vector.tensor_copy(
+                g_pick[:, PACK - 1, lo:hi], g_in[PACK - 1][:].indirect(offsets[:, lo // 16 : hi // 16])
+            )
         for i in range(TILES):
             pick_last(i)
         product_d(0)
@@ -248,7 +249,7 @@ def tile_moe_expert_back_made_anew_pl_kernel(
             place(t, lo, J, product_p(t, EARLY)[:, lo:J], "p_rows%d" % t)
             if t < PACK - 1:
                 y_t = y_pair[t // 2][:, t % 2, :]
-                nc.vector.tensor_tensor(out=y_t, in0=placed[t][:], in1=run_in[t][:], op=ALU.add)
+                nc.gpsimd.tensor_tensor(out=y_t, in0=placed[t][:], in1=run_in[t][:], op=ALU.add)
                 nc.sync.dma_start(out=out_rows[t], in_=y_t)
             if t == 1:
                 for c in range(CHUNKS):

@@ -20,11 +20,14 @@ ACT = mybir.ActivationFunctionType
 
 P = 128
 PACK = 4
+QUADS = 4
+PER_COLUMN = 16
 TOK = 128
-TILES = J // TOK
+GROUPS = J // TOK
 EARLY = 2 * TOK
 CHUNK = 256
 CHUNKS = T // CHUNK
+SPLIT = 640
 
 
 def tile_moe_expert_back_made_anew_pl_kernel(
@@ -36,55 +39,60 @@ def tile_moe_expert_back_made_anew_pl_kernel(
         keep = ctx.enter_context(tc.tile_pool(name="keep", bufs=1))
         psum = ctx.enter_context(tc.psum_pool(name="psum", bufs=2))
 
-        def load_scales_everywhere(plane, rows):
-            for q in range(4):
+        def load_scales(dest, rows):
+            for quad in range(QUADS):
                 nc.sync.dma_start(
-                    out=plane[32 * q : 32 * q + 32, :].bitcast(I32),
-                    in_=rows[0, 4 * q : 4 * q + 4, :].bitcast(I32).partition_broadcast(8),
+                    out=dest[32 * quad : 32 * quad + 4, :].bitcast(I32),
+                    in_=rows[0, 4 * quad : 4 * quad + 4, :].bitcast(I32),
                 )
 
-        offsets = keep.tile([P, J // 16], U16, name="offsets")
+        offsets = keep.tile([P, J // PER_COLUMN], U16, name="offsets")
         xt_w = keep.tile([P, 2 * T], U8, name="xt_w", align_bytes=64)
         xt_s = keep.tile([P, T], U8, name="xt_s", align_bytes=64)
-        w_s = keep.tile([P, 2 * R], U8, name="w_s", align_bytes=64)
-        wa_s, wd_s = (w_s[:, i * R : (i + 1) * R] for i in range(2))
-        wu_s = keep.tile([P, K], U8, name="wu_s", align_bytes=64)
+        w_s = keep.tile([P, 3 * R], U8, name="w_s", align_bytes=64)
+        wa_s, wd_s, wu_s = (w_s[:, i * R : (i + 1) * R] for i in range(3))
         wa_w = keep.tile([P, R], U32, name="wa_w", align_bytes=64)
         wd_w = keep.tile([P, 2 * R], U8, name="wd_w", align_bytes=64)
         wu_w = keep.tile([P, K], I32, name="wu_w", align_bytes=64)
-        g_rows = g.rearrange("(p t) c -> t p c", t=PACK)
-        run_rows = run.rearrange("(p t) c -> t p c", t=PACK)
-        out_rows = out_0.rearrange("(p t) c -> t p c", t=PACK)
+        g_slices = g.rearrange("(p t) c -> t p c", t=PACK)
+        run_slices = run.rearrange("(p t) c -> t p c", t=PACK)
+        out_slices = out_0.rearrange("(p t) c -> t p c", t=PACK)
         g_in = [keep.tile([P, T], F32, name="g_in%d" % t) for t in range(PACK)]
         run_in = [keep.tile([P, T], F32, name="run_in%d" % t) for t in range(PACK)]
 
+        def entries(lo, hi):
+            return offsets[:, lo // PER_COLUMN : hi // PER_COLUMN]
+
+        nc.vector.memset(xt_s[:].bitcast(I32), 0)
+        nc.vector.memset(w_s[:].bitcast(I32), 0)
 
         nc.sync.dma_start(offsets[:], offs)
-        load_scales_everywhere(xt_s, xt_scales)
         nc.sync.dma_start(out=xt_w[:].bitcast(I32), in_=xt_words[0].bitcast(I32))
+        load_scales(xt_s, xt_scales)
+        for t in range(2):
+            nc.sync.dma_start(out=g_in[t][:], in_=g_slices[t])
         nc.sync.dma_start(out=wa_w[:].bitcast(I32), in_=wa_words[0].rearrange("p c r -> p (c r)").bitcast(I32))
-        nc.sync.dma_start(out=g_in[0][:], in_=g_rows[0])
-        load_scales_everywhere(wa_s, wa_scales)
-        for t in range(1, PACK):
-            nc.sync.dma_start(out=g_in[t][:], in_=g_rows[t])
+        load_scales(wa_s, wa_scales)
+        for t in range(2, PACK):
+            nc.sync.dma_start(out=g_in[t][:], in_=g_slices[t])
+        load_scales(wd_s, wd_scales)
         nc.sync.dma_start(out=wd_w[:].bitcast(I32), in_=wd_words[0].bitcast(I32))
-        load_scales_everywhere(wd_s, wd_scales)
         nc.sync.dma_start(out=wu_w[:], in_=wu_words[0].rearrange("p c r -> p (c r)").bitcast(I32))
-        load_scales_everywhere(wu_s, wu_scales)
+        load_scales(wu_s, wu_scales)
         for t in range(PACK):
-            nc.sync.dma_start(out=run_in[t][:], in_=run_rows[t])
+            nc.sync.dma_start(out=run_in[t][:], in_=run_slices[t])
 
         ident = keep.tile([P, P], F32, name="ident")
         make_identity(nc, ident[:])
 
-        placed = [keep.tile([P, T], F32, name="placed%d" % t) for t in range(PACK - 1)]
-        for t in range(PACK - 1):
-            nc.vector.memset(placed[t][:], 0.0)
+        placed = [keep.tile([P, T], F32, name="placed%d" % t) for t in range(PACK)]
+        for t in range(PACK):
+            nc.gpsimd.memset(placed[t][:], 0.0)
 
         xg_w = keep.tile([P, 2 * J], U8, name="xg_w", align_bytes=64)
         xg_s = keep.tile([P, J], U8, name="xg_s", align_bytes=64)
-        nc.vector.tensor_copy(xg_s[:], xt_s[:].indirect(offsets[:]))
         nc.vector.tensor_copy(xg_w[:].bitcast(U16), xt_w[:].bitcast(U16).indirect(offsets[:]))
+        nc.vector.tensor_copy(xg_s[:], xt_s[:].indirect(offsets[:]))
 
         g_pick = keep.tile([P, PACK, J], BF16, name="g_pick", align_bytes=64)
         g_round = keep.tile([P, T], BF16, name="g_round", align_bytes=64)
@@ -93,8 +101,7 @@ def tile_moe_expert_back_made_anew_pl_kernel(
 
         relu2 = {}
 
-        def product_a(i):
-            tag = "relu2_%d" % i if i < 2 else "g_woven%d" % (i - 2)
+        def product_a(i, tag):
             relu2[i] = keep.tile([P, R], F32, name="relu2_%d" % i, tag=tag, align_bytes=64)
             a_ps = psum.tile([P, R], F32, name="a_ps")
             nc.tensor.matmul_mx(
@@ -106,15 +113,10 @@ def tile_moe_expert_back_made_anew_pl_kernel(
                 start=True,
                 stop=True,
             )
-            nc.scalar.activation(
-                out=relu2[i][:],
-                in_=a_ps[:],
-                func=ACT.Relu,
-                scale=2.0,
-            )
+            nc.scalar.activation(out=relu2[i][:], in_=a_ps[:], func=ACT.Relu, scale=2.0)
 
-        product_a(0)
-        product_a(1)
+        product_a(0, "relu2_0")
+        product_a(1, "relu2_1")
 
         for t in range(1, PACK - 1):
             nc.vector.tensor_copy(g_pick[:, t, :], g_in[t][:].indirect(offsets[:]))
@@ -124,21 +126,27 @@ def tile_moe_expert_back_made_anew_pl_kernel(
         dz_scales = keep.tile([P, EARLY + J], U8, name="dz_scales", align_bytes=64)
         nc.vector.memset(dz_codes[:, 0:EARLY].bitcast(I32), 0)
         nc.vector.memset(dz_scales[:, 0:EARLY].bitcast(I32), 0)
-        g_woven = [keep.tile([P, TOK, PACK], BF16, name="g_woven%d" % i, tag="g_woven%d" % i, align_bytes=64) for i in range(TILES)]
-        dz_rows = [keep.tile([P, R], BF16, name="dz_rows%d" % i, tag="dz_rows%d" % i, align_bytes=64) for i in range(TILES)]
-        dz_woven = [keep.tile([P, TOK * PACK], BF16, name="dz_woven%d" % i, tag="dz_woven%d" % i, align_bytes=64) for i in range(TILES)]
+        g_woven = [
+            keep.tile([P, TOK, PACK], BF16, name="g_woven%d" % i, tag="g_woven%d" % i, align_bytes=64)
+            for i in range(GROUPS)
+        ]
+        dz_rows = [
+            keep.tile([P, R], BF16, name="dz_rows%d" % i, tag="dz_rows%d" % i, align_bytes=64) for i in range(GROUPS)
+        ]
+        dz_woven = [
+            keep.tile([P, TOK * PACK], BF16, name="dz_woven%d" % i, tag="dz_woven%d" % i, align_bytes=64)
+            for i in range(GROUPS)
+        ]
         d_ps = {}
 
-        def pick_last(i):
-            cols = slice(TOK * i, TOK * (i + 1))
+        def weave_g(i):
             nc.scalar.copy(
-                out=g_woven[i][:].rearrange("p (c n) t -> p c t n", n=4),
-                in_=g_pick[:, :, cols].rearrange("p t (c n) -> p c t n", n=4),
+                out=g_woven[i][:].rearrange("p (c e) t -> p c t e", e=4),
+                in_=g_pick[:, :, TOK * i : TOK * (i + 1)].rearrange("p t (c e) -> p c t e", e=4),
             )
 
-        def product_d(i):
+        def product_d(i, tag):
             cols = slice(TOK * i, TOK * (i + 1))
-            tag = "g_codes%d" % i if i < 2 else "relu2_%d" % (i - 2)
             g_codes = keep.tile([P, TOK], U32, name="g_codes%d" % i, tag=tag, align_bytes=64)
             nc.vector.quantize_mx(
                 out=g_codes[:].bitcast(E5M2),
@@ -157,16 +165,11 @@ def tile_moe_expert_back_made_anew_pl_kernel(
             )
 
         def make_dz(i):
-            nc.vector.tensor_tensor(
-                out=dz_rows[i][:],
-                in0=d_ps[i][:],
-                in1=relu2[i][:],
-                op=ALU.mult,
-            )
+            nc.vector.tensor_tensor(out=dz_rows[i][:], in0=d_ps[i][:], in1=relu2[i][:], op=ALU.mult)
             turned = psum.tile([P, 2, TOK], F32, name="turned")
-            words = dz_rows[i][:].bitcast(F32)
+            pairs = dz_rows[i][:].bitcast(F32)
             for u in range(2):
-                nc.tensor.transpose(turned[:, u, :], words[:, u : 2 * P : 2], ident[:])
+                nc.tensor.transpose(turned[:, u, :], pairs[:, u : 2 * P : 2], ident[:])
             nc.scalar.copy(
                 out=dz_woven[i][:].bitcast(F32).rearrange("p (j u) -> p j u", u=2),
                 in_=turned[:].rearrange("p u j -> p j u"),
@@ -176,26 +179,23 @@ def tile_moe_expert_back_made_anew_pl_kernel(
             cols = slice(EARLY + TOK * i, EARLY + TOK * (i + 1))
             nc.vector.quantize_mx(out=dz_codes[:, cols].bitcast(E5M2), scales=dz_scales[:, cols], in_=dz_woven[i][:])
 
-        wu_dealt = {}
-
         def deal_wu():
-            wu_wp = keep.tile([P, K], I32, name="wu_wp", align_bytes=64)
-            wu_sp = keep.tile([P, K], U8, name="wu_sp", align_bytes=64)
+            words = keep.tile([P, K], I32, name="wu_dealt_w", align_bytes=64)
+            scales = keep.tile([P, K], U8, name="wu_dealt_s", align_bytes=64)
             nc.vector.tensor_copy(
-                out=wu_wp[:].rearrange("p (t m) -> p m t", t=PACK), in_=wu_w[:].rearrange("p (m t) -> p m t", t=PACK)
+                out=words[:].rearrange("p (t m) -> p m t", t=PACK), in_=wu_w[:].rearrange("p (m t) -> p m t", t=PACK)
             )
             nc.vector.tensor_copy(
-                out=wu_sp[:].rearrange("p (t m) -> p m t", t=PACK), in_=wu_s[:].rearrange("p (m t) -> p m t", t=PACK)
+                out=scales[:].rearrange("p (t m) -> p m t", t=PACK), in_=wu_s.rearrange("p (m t) -> p m t", t=PACK)
             )
-            wu_dealt["words"] = wu_wp
-            wu_dealt["scales"] = wu_sp
+            return words, scales
 
         def product_p(t, first):
             p_ps = psum.tile([P, J], F32, name="p_ps")
             nc.tensor.matmul_mx(
                 out=p_ps[:],
-                lhsT=wu_dealt["words"][:, P * t : P * (t + 1)].bitcast(E4M3),
-                lhsT_scale=wu_dealt["scales"][:, P * t : P * (t + 1)],
+                lhsT=wu_dealt_w[:, P * t : P * (t + 1)].bitcast(E4M3),
+                lhsT_scale=wu_dealt_s[:, P * t : P * (t + 1)],
                 rhs=dz_codes[:, first : first + J].bitcast(E5M2),
                 rhs_scale=dz_scales[:, first : first + J],
                 start=True,
@@ -204,80 +204,81 @@ def tile_moe_expert_back_made_anew_pl_kernel(
             return p_ps
 
         def place(t, lo, hi, sums, tag):
-            rows = keep.tile([P, hi - lo], F32, name="p_rows%d_%d" % (t, lo), tag=tag, align_bytes=64)
-            nc.scalar.copy(out=rows[:], in_=sums)
-            nc.vector.tensor_copy(placed[t][:].indirect(offsets[:, lo // 16 : hi // 16]), rows[:])
+            staged = keep.tile([P, hi - lo], F32, name="p_staged%d_%d" % (t, lo), tag=tag, align_bytes=64)
+            nc.scalar.copy(out=staged[:], in_=sums)
+            nc.vector.tensor_copy(placed[t][:].indirect(entries(lo, hi)), staged[:])
 
         for lo, hi in ((0, TOK), (TOK, J)):
-            nc.vector.tensor_copy(
-                g_pick[:, PACK - 1, lo:hi], g_in[PACK - 1][:].indirect(offsets[:, lo // 16 : hi // 16])
-            )
-        for i in range(TILES):
-            pick_last(i)
-        product_d(0)
-        product_a(2)
-        product_d(1)
-        product_a(3)
-        deal_wu()
-        make_dz(0)
-        product_d(2)
-        make_dz(1)
-        product_d(3)
+            nc.vector.tensor_copy(g_pick[:, PACK - 1, lo:hi], g_in[PACK - 1][:].indirect(entries(lo, hi)))
+        for i in range(GROUPS):
+            weave_g(i)
+
+        for i in range(2):
+            product_d(i, "g_codes%d" % i)
+            product_a(i + 2, "g_woven%d" % i)
+        wu_dealt_w, wu_dealt_s = deal_wu()
+        for i in range(2):
+            make_dz(i)
+            product_d(i + 2, "relu2_%d" % i)
         quantize_dz(0)
         make_dz(2)
         quantize_dz(1)
-        early = product_p(0, 0)
+
+        early = [product_p(t, 0) for t in range(2)]
         make_dz(3)
         quantize_dz(2)
-        place(0, 0, TOK, early[:, EARLY : EARLY + TOK], "p_first")
+        place(0, 0, TOK, early[0][:, EARLY : EARLY + TOK], "p_first")
         quantize_dz(3)
-        placed.append(keep.tile([P, T], F32, name="placed3", tag="dz_woven3", align_bytes=64))
-        nc.vector.memset(placed[3][:], 0.0)
-        place(0, TOK, EARLY, early[:, EARLY + TOK : J], "dz_rows3")
+        place(0, TOK, EARLY, early[0][:, EARLY + TOK : J], "dz_rows3")
+        place(1, 0, EARLY, early[1][:, EARLY:J], "dz_woven3")
 
         y_pair = [keep.tile([P, 2, T], F32, name="y_pair%d" % h) for h in range(2)]
         y_woven = [keep.tile([P, CHUNK, PACK], BF16, name="y_woven%d" % c, align_bytes=64) for c in range(CHUNKS)]
         y_codes = keep.tile([P, T], U32, name="y_codes", align_bytes=64)
         y_scales = keep.tile([P, T], U8, name="y_scales", align_bytes=64)
 
-        def weave_pair(engine_copy, h, c):
-            cols = slice(CHUNK * c, CHUNK * (c + 1))
-            engine_copy(out=y_woven[c][:, :, 2 * h : 2 * h + 2], in_=y_pair[h][:, :, cols].rearrange("p t c -> p c t"))
-
-        for t in range(PACK):
-            lo = EARLY if t == 0 else 0
-            place(t, lo, J, product_p(t, EARLY)[:, lo:J], "p_rows%d" % t)
-            if t < PACK - 1:
-                y_t = y_pair[t // 2][:, t % 2, :]
-                nc.gpsimd.tensor_tensor(out=y_t, in0=placed[t][:], in1=run_in[t][:], op=ALU.add)
-                nc.sync.dma_start(out=out_rows[t], in_=y_t)
-            if t == 1:
-                for c in range(CHUNKS):
-                    weave_pair(nc.scalar.copy, 0, c)
+        def weave_pair(engine_copy, h, lo, hi):
+            c = lo // CHUNK
+            engine_copy(
+                out=y_woven[c][:, lo - CHUNK * c : hi - CHUNK * c, 2 * h : 2 * h + 2],
+                in_=y_pair[h][:, :, lo:hi].rearrange("p e col -> p col e"),
+            )
 
         last = PACK - 1
-        for c in range(CHUNKS):
-            cols = slice(CHUNK * c, CHUNK * (c + 1))
+        for t in range(PACK):
+            lo = EARLY if t < len(early) else 0
+            place(t, lo, J, product_p(t, EARLY)[:, lo:J], "p_staged%d" % t)
+            if t < last:
+                y_slice = y_pair[t // 2][:, t % 2, :]
+                nc.gpsimd.tensor_tensor(out=y_slice, in0=placed[t][:], in1=run_in[t][:], op=ALU.add)
+                nc.sync.dma_start(out=out_slices[t], in_=y_slice)
+            if t == 1:
+                for c in range(CHUNKS):
+                    weave_pair(nc.scalar.copy, 0, CHUNK * c, CHUNK * (c + 1))
+
+        for lo, hi in ((0, CHUNK), (CHUNK, SPLIT), (SPLIT, T)):
             nc.vector.tensor_tensor(
-                out=y_pair[1][:, 1, cols], in0=placed[last][:, cols], in1=run_in[last][:, cols], op=ALU.add
+                out=y_pair[1][:, 1, lo:hi], in0=placed[last][:, lo:hi], in1=run_in[last][:, lo:hi], op=ALU.add
             )
-            if c % 2 == 1:
-                half = slice(CHUNK * (c - 1), CHUNK * (c + 1))
-                nc.sync.dma_start(out=out_rows[last][:, half], in_=y_pair[1][:, 1, half])
-        for c in range(CHUNKS):
-            weave_pair(nc.scalar.copy if c < CHUNKS // 2 else nc.vector.tensor_copy, 1, c)
+        for lo, hi in ((0, SPLIT), (SPLIT, T)):
+            nc.sync.dma_start(out=out_slices[last][:, lo:hi], in_=y_pair[1][:, 1, lo:hi])
+        for lo, hi in ((0, CHUNK), (CHUNK, 2 * CHUNK), (2 * CHUNK, SPLIT)):
+            weave_pair(nc.scalar.copy, 1, lo, hi)
+        for lo, hi in ((SPLIT, 3 * CHUNK), (3 * CHUNK, T)):
+            weave_pair(nc.vector.tensor_copy, 1, lo, hi)
 
         words_out = out_1[0].rearrange("p c r -> p (c r)").bitcast(I32)
-        for c in (0, 2, 3, 1):
+        for c in (0, 3, 1, 2):
             cols = slice(CHUNK * c, CHUNK * (c + 1))
             nc.vector.quantize_mx(
                 out=y_codes[:, cols].bitcast(E4M3),
                 scales=y_scales[:, cols],
-                in_=y_woven[c][:].rearrange("p c t -> p (c t)"),
+                in_=y_woven[c][:].rearrange("p col t -> p (col t)"),
             )
             nc.sync.dma_start(out=words_out[:, cols], in_=y_codes[:, cols].bitcast(I32))
-        for q in range(4):
-            queue = nc.sync if q % 2 == 0 else nc.scalar
+        for quad in range(QUADS):
+            queue = nc.sync if quad % 2 == 0 else nc.scalar
             queue.dma_start(
-                out=out_2[0, 4 * q : 4 * q + 4, :].bitcast(I32), in_=y_scales[32 * q : 32 * q + 4, :].bitcast(I32)
+                out=out_2[0, 4 * quad : 4 * quad + 4, :].bitcast(I32),
+                in_=y_scales[32 * quad : 32 * quad + 4, :].bitcast(I32),
             )

from contextlib import ExitStack

import concourse.mybir as mybir
from concourse.masks import make_identity

K, R, N, T, J = 512, 512, 512, 1024, 512
FLOPS = 2 * J * (K * R + N * R + R * K)

F32 = mybir.dt.float32
BF16 = mybir.dt.bfloat16
I32 = mybir.dt.int32
U32 = mybir.dt.uint32
U16 = mybir.dt.uint16
U8 = mybir.dt.uint8
E4M3 = mybir.dt.float8_e4m3fn_x4
E5M2 = mybir.dt.float8_e5m2_x4
E2M1 = mybir.dt.float4_e2m1fn_x4
ALU = mybir.AluOpType
ACT = mybir.ActivationFunctionType

P = 128
PACK = 4
QUADS = 4
PER_COLUMN = 16
TOK = 128
GROUPS = J // TOK
EARLY = 2 * TOK
CHUNK = 256
CHUNKS = T // CHUNK
SPLIT = 640


def tile_moe_expert_back_made_anew_pl_kernel(
    tc, xt_words, xt_scales, wa_words, wa_scales, g, wd_words, wd_scales, wu_words, wu_scales, run, offs,
    out_0, out_1, out_2,
):
    nc = tc.nc
    with ExitStack() as ctx:
        keep = ctx.enter_context(tc.tile_pool(name="keep", bufs=1))
        psum = ctx.enter_context(tc.psum_pool(name="psum", bufs=2))

        def load_scales(dest, rows):
            for quad in range(QUADS):
                nc.sync.dma_start(
                    out=dest[32 * quad : 32 * quad + 4, :].bitcast(I32),
                    in_=rows[0, 4 * quad : 4 * quad + 4, :].bitcast(I32),
                )

        offsets = keep.tile([P, J // PER_COLUMN], U16, name="offsets")
        xt_w = keep.tile([P, 2 * T], U8, name="xt_w", align_bytes=64)
        xt_s = keep.tile([P, T], U8, name="xt_s", align_bytes=64)
        w_s = keep.tile([P, 3 * R], U8, name="w_s", align_bytes=64)
        wa_s, wd_s, wu_s = (w_s[:, i * R : (i + 1) * R] for i in range(3))
        wa_w = keep.tile([P, R], U32, name="wa_w", align_bytes=64)
        wd_w = keep.tile([P, 2 * R], U8, name="wd_w", align_bytes=64)
        wu_w = keep.tile([P, K], I32, name="wu_w", align_bytes=64)
        g_slices = g.rearrange("(p t) c -> t p c", t=PACK)
        run_slices = run.rearrange("(p t) c -> t p c", t=PACK)
        out_slices = out_0.rearrange("(p t) c -> t p c", t=PACK)
        g_in = [keep.tile([P, T], F32, name="g_in%d" % t) for t in range(PACK)]
        run_in = [keep.tile([P, T], F32, name="run_in%d" % t) for t in range(PACK)]

        def entries(lo, hi):
            return offsets[:, lo // PER_COLUMN : hi // PER_COLUMN]

        nc.vector.memset(xt_s[:].bitcast(I32), 0)
        nc.vector.memset(w_s[:].bitcast(I32), 0)

        nc.sync.dma_start(offsets[:], offs)
        nc.sync.dma_start(out=xt_w[:].bitcast(I32), in_=xt_words[0].bitcast(I32))
        load_scales(xt_s, xt_scales)
        for t in range(2):
            nc.sync.dma_start(out=g_in[t][:], in_=g_slices[t])
        nc.sync.dma_start(out=wa_w[:].bitcast(I32), in_=wa_words[0].rearrange("p c r -> p (c r)").bitcast(I32))
        load_scales(wa_s, wa_scales)
        for t in range(2, PACK):
            nc.sync.dma_start(out=g_in[t][:], in_=g_slices[t])
        load_scales(wd_s, wd_scales)
        nc.sync.dma_start(out=wd_w[:].bitcast(I32), in_=wd_words[0].bitcast(I32))
        nc.sync.dma_start(out=wu_w[:], in_=wu_words[0].rearrange("p c r -> p (c r)").bitcast(I32))
        load_scales(wu_s, wu_scales)
        for t in range(PACK):
            nc.sync.dma_start(out=run_in[t][:], in_=run_slices[t])

        ident = keep.tile([P, P], F32, name="ident")
        make_identity(nc, ident[:])

        placed = [keep.tile([P, T], F32, name="placed%d" % t) for t in range(PACK)]
        for t in range(PACK):
            nc.gpsimd.memset(placed[t][:], 0.0)

        xg_w = keep.tile([P, 2 * J], U8, name="xg_w", align_bytes=64)
        xg_s = keep.tile([P, J], U8, name="xg_s", align_bytes=64)
        nc.vector.tensor_copy(xg_w[:].bitcast(U16), xt_w[:].bitcast(U16).indirect(offsets[:]))
        nc.vector.tensor_copy(xg_s[:], xt_s[:].indirect(offsets[:]))

        g_pick = keep.tile([P, PACK, J], BF16, name="g_pick", align_bytes=64)
        g_round = keep.tile([P, T], BF16, name="g_round", align_bytes=64)
        nc.scalar.activation(out=g_round[:], in_=g_in[0][:], func=ACT.Copy)
        nc.scalar.activation(out=g_pick[:, 0, :], in_=g_round[:].indirect(offsets[:]), func=ACT.Copy)

        relu2 = {}

        def product_a(i, tag):
            relu2[i] = keep.tile([P, R], F32, name="relu2_%d" % i, tag=tag, align_bytes=64)
            a_ps = psum.tile([P, R], F32, name="a_ps")
            nc.tensor.matmul_mx(
                out=a_ps[:],
                lhsT=xg_w[:, 2 * TOK * i : 2 * TOK * (i + 1)].bitcast(E2M1),
                lhsT_scale=xg_s[:, TOK * i : TOK * (i + 1)],
                rhs=wa_w[:].bitcast(E4M3),
                rhs_scale=wa_s,
                start=True,
                stop=True,
            )
            nc.scalar.activation(out=relu2[i][:], in_=a_ps[:], func=ACT.Relu, scale=2.0)

        product_a(0, "relu2_0")
        product_a(1, "relu2_1")

        for t in range(1, PACK - 1):
            nc.vector.tensor_copy(g_pick[:, t, :], g_in[t][:].indirect(offsets[:]))

        g_scales = keep.tile([P, J], U8, name="g_scales", align_bytes=64)
        dz_codes = keep.tile([P, EARLY + J], U32, name="dz_codes", align_bytes=64)
        dz_scales = keep.tile([P, EARLY + J], U8, name="dz_scales", align_bytes=64)
        nc.vector.memset(dz_codes[:, 0:EARLY].bitcast(I32), 0)
        nc.vector.memset(dz_scales[:, 0:EARLY].bitcast(I32), 0)
        g_woven = [
            keep.tile([P, TOK, PACK], BF16, name="g_woven%d" % i, tag="g_woven%d" % i, align_bytes=64)
            for i in range(GROUPS)
        ]
        dz_rows = [
            keep.tile([P, R], BF16, name="dz_rows%d" % i, tag="dz_rows%d" % i, align_bytes=64) for i in range(GROUPS)
        ]
        dz_woven = [
            keep.tile([P, TOK * PACK], BF16, name="dz_woven%d" % i, tag="dz_woven%d" % i, align_bytes=64)
            for i in range(GROUPS)
        ]
        d_ps = {}

        def weave_g(i):
            nc.scalar.copy(
                out=g_woven[i][:].rearrange("p (c e) t -> p c t e", e=4),
                in_=g_pick[:, :, TOK * i : TOK * (i + 1)].rearrange("p t (c e) -> p c t e", e=4),
            )

        def product_d(i, tag):
            cols = slice(TOK * i, TOK * (i + 1))
            g_codes = keep.tile([P, TOK], U32, name="g_codes%d" % i, tag=tag, align_bytes=64)
            nc.vector.quantize_mx(
                out=g_codes[:].bitcast(E5M2),
                scales=g_scales[:, cols],
                in_=g_woven[i][:].rearrange("p j t -> p (j t)"),
            )
            d_ps[i] = psum.tile([P, R], F32, name="d_ps")
            nc.tensor.matmul_mx(
                out=d_ps[i][:],
                lhsT=g_codes[:].bitcast(E5M2),
                lhsT_scale=g_scales[:, cols],
                rhs=wd_w[:].bitcast(E2M1),
                rhs_scale=wd_s,
                start=True,
                stop=True,
            )

        def make_dz(i):
            nc.vector.tensor_tensor(out=dz_rows[i][:], in0=d_ps[i][:], in1=relu2[i][:], op=ALU.mult)
            turned = psum.tile([P, 2, TOK], F32, name="turned")
            pairs = dz_rows[i][:].bitcast(F32)
            for u in range(2):
                nc.tensor.transpose(turned[:, u, :], pairs[:, u : 2 * P : 2], ident[:])
            nc.scalar.copy(
                out=dz_woven[i][:].bitcast(F32).rearrange("p (j u) -> p j u", u=2),
                in_=turned[:].rearrange("p u j -> p j u"),
            )

        def quantize_dz(i):
            cols = slice(EARLY + TOK * i, EARLY + TOK * (i + 1))
            nc.vector.quantize_mx(out=dz_codes[:, cols].bitcast(E5M2), scales=dz_scales[:, cols], in_=dz_woven[i][:])

        def deal_wu():
            words = keep.tile([P, K], I32, name="wu_dealt_w", align_bytes=64)
            scales = keep.tile([P, K], U8, name="wu_dealt_s", align_bytes=64)
            nc.vector.tensor_copy(
                out=words[:].rearrange("p (t m) -> p m t", t=PACK), in_=wu_w[:].rearrange("p (m t) -> p m t", t=PACK)
            )
            nc.vector.tensor_copy(
                out=scales[:].rearrange("p (t m) -> p m t", t=PACK), in_=wu_s.rearrange("p (m t) -> p m t", t=PACK)
            )
            return words, scales

        def product_p(t, first):
            p_ps = psum.tile([P, J], F32, name="p_ps")
            nc.tensor.matmul_mx(
                out=p_ps[:],
                lhsT=wu_dealt_w[:, P * t : P * (t + 1)].bitcast(E4M3),
                lhsT_scale=wu_dealt_s[:, P * t : P * (t + 1)],
                rhs=dz_codes[:, first : first + J].bitcast(E5M2),
                rhs_scale=dz_scales[:, first : first + J],
                start=True,
                stop=True,
            )
            return p_ps

        def place(t, lo, hi, sums, tag):
            staged = keep.tile([P, hi - lo], F32, name="p_staged%d_%d" % (t, lo), tag=tag, align_bytes=64)
            nc.scalar.copy(out=staged[:], in_=sums)
            nc.vector.tensor_copy(placed[t][:].indirect(entries(lo, hi)), staged[:])

        for lo, hi in ((0, TOK), (TOK, J)):
            nc.vector.tensor_copy(g_pick[:, PACK - 1, lo:hi], g_in[PACK - 1][:].indirect(entries(lo, hi)))
        for i in range(GROUPS):
            weave_g(i)

        for i in range(2):
            product_d(i, "g_codes%d" % i)
            product_a(i + 2, "g_woven%d" % i)
        wu_dealt_w, wu_dealt_s = deal_wu()
        for i in range(2):
            make_dz(i)
            product_d(i + 2, "relu2_%d" % i)
        quantize_dz(0)
        make_dz(2)
        quantize_dz(1)

        early = [product_p(t, 0) for t in range(2)]
        make_dz(3)
        quantize_dz(2)
        place(0, 0, TOK, early[0][:, EARLY : EARLY + TOK], "p_first")
        quantize_dz(3)
        place(0, TOK, EARLY, early[0][:, EARLY + TOK : J], "dz_rows3")
        place(1, 0, EARLY, early[1][:, EARLY:J], "dz_woven3")

        y_pair = [keep.tile([P, 2, T], F32, name="y_pair%d" % h) for h in range(2)]
        y_woven = [keep.tile([P, CHUNK, PACK], BF16, name="y_woven%d" % c, align_bytes=64) for c in range(CHUNKS)]
        y_codes = keep.tile([P, T], U32, name="y_codes", align_bytes=64)
        y_scales = keep.tile([P, T], U8, name="y_scales", align_bytes=64)

        def weave_pair(engine_copy, h, lo, hi):
            c = lo // CHUNK
            engine_copy(
                out=y_woven[c][:, lo - CHUNK * c : hi - CHUNK * c, 2 * h : 2 * h + 2],
                in_=y_pair[h][:, :, lo:hi].rearrange("p e col -> p col e"),
            )

        last = PACK - 1
        for t in range(PACK):
            lo = EARLY if t < len(early) else 0
            place(t, lo, J, product_p(t, EARLY)[:, lo:J], "p_staged%d" % t)
            if t < last:
                y_slice = y_pair[t // 2][:, t % 2, :]
                nc.gpsimd.tensor_tensor(out=y_slice, in0=placed[t][:], in1=run_in[t][:], op=ALU.add)
                nc.sync.dma_start(out=out_slices[t], in_=y_slice)
            if t == 1:
                for c in range(CHUNKS):
                    weave_pair(nc.scalar.copy, 0, CHUNK * c, CHUNK * (c + 1))

        for lo, hi in ((0, CHUNK), (CHUNK, SPLIT), (SPLIT, T)):
            nc.vector.tensor_tensor(
                out=y_pair[1][:, 1, lo:hi], in0=placed[last][:, lo:hi], in1=run_in[last][:, lo:hi], op=ALU.add
            )
        for lo, hi in ((0, SPLIT), (SPLIT, T)):
            nc.sync.dma_start(out=out_slices[last][:, lo:hi], in_=y_pair[1][:, 1, lo:hi])
        for lo, hi in ((0, CHUNK), (CHUNK, 2 * CHUNK), (2 * CHUNK, SPLIT)):
            weave_pair(nc.scalar.copy, 1, lo, hi)
        for lo, hi in ((SPLIT, 3 * CHUNK), (3 * CHUNK, T)):
            weave_pair(nc.vector.tensor_copy, 1, lo, hi)

        words_out = out_1[0].rearrange("p c r -> p (c r)").bitcast(I32)
        for c in (0, 3, 1, 2):
            cols = slice(CHUNK * c, CHUNK * (c + 1))
            nc.vector.quantize_mx(
                out=y_codes[:, cols].bitcast(E4M3),
                scales=y_scales[:, cols],
                in_=y_woven[c][:].rearrange("p col t -> p (col t)"),
            )
            nc.sync.dma_start(out=words_out[:, cols], in_=y_codes[:, cols].bitcast(I32))
        for quad in range(QUADS):
            queue = nc.sync if quad % 2 == 0 else nc.scalar
            queue.dma_start(
                out=out_2[0, 4 * quad : 4 * quad + 4, :].bitcast(I32),
                in_=y_scales[32 * quad : 32 * quad + 4, :].bitcast(I32),
            )
